import numpy as np
import ml_dtypes


def mxq(x, axis, fmt="e4m3"):
    dtype, down = {"e4m3": (ml_dtypes.float8_e4m3fn, 7), "e5m2": (ml_dtypes.float8_e5m2, 14)}[fmt]
    v = np.moveaxis(np.asarray(x, np.float32).astype(ml_dtypes.bfloat16).astype(np.float64), axis, -1)
    blocks = v.reshape(v.shape[:-1] + (-1, 32))
    amax = np.abs(blocks).max(-1, keepdims=True)
    byte = np.maximum(np.where(amax > 0, np.frexp(amax)[1] - 1 + 127, 0) - down, 1)
    scale = np.exp2(byte - 127.0)
    codes = (blocks / scale).astype(np.float32).astype(dtype).astype(np.float64)
    return np.moveaxis((codes * scale).reshape(v.shape), -1, axis)


WIDE = False


def mx_kscale(k):
    if not WIDE:
        return np.ones(k)
    levels = np.array([30, -30])
    if k % 512:
        return np.exp2(np.random.permutation(np.resize(levels, k // 32))).repeat(32)
    a = np.empty((k // 512, 16))
    for p in range(k // 512):
        a[p, :8] = np.random.permutation(np.resize(levels, 8))
        for g in range(8):
            far = levels[np.abs(levels - a[p, g]) >= 10]
            a[p, g + 8] = far[np.random.randint(len(far))]
    return np.exp2(a.ravel()).repeat(32)


def f64(x):
    return np.asarray(x).astype(np.float64)


def striped(idx):
    return np.tile(np.asarray(idx).reshape(-1, 16).T, (8, 1)).astype(np.uint16)


def unstriped(offs):
    return offs[:16].T.reshape(-1).astype(np.int64)


E2M1 = np.array([0.0, 0.5, 1.0, 1.5, 2.0, 3.0, 4.0, 6.0, -0.0, -0.5, -1.0, -1.5, -2.0, -3.0, -4.0, -6.0])


def pack_weight(w, fmt):
    k, n = w.shape
    w = f64(np.asarray(w, np.float32).astype(ml_dtypes.bfloat16)).reshape(k // 32, 32, n)
    amax = np.abs(w).max(1)
    if fmt in ("e4m3", "e5m2"):
        byte = np.frexp(amax)[1] - 1 + 127 - (7 if fmt == "e4m3" else 14)
    else:
        mant, ex = np.frexp(amax / 6.0)
        byte = np.where(mant > 0.5, ex, ex - 1) + 127
    byte = np.clip(np.where(amax > 0, byte, 1), 1, 254)
    scaled = (w * np.exp2(127.0 - byte)[:, None, :]).reshape(k, n).astype(np.float32)
    by_word = np.ascontiguousarray(scaled.reshape(k // 512, 128, 4, n).transpose(0, 1, 3, 2))
    if fmt in ("e4m3", "e5m2"):
        words = by_word.astype(ml_dtypes.float8_e4m3fn if fmt == "e4m3" else ml_dtypes.float8_e5m2).view(np.uint8)
    else:
        c = by_word.astype(ml_dtypes.float4_e2m1fn).view(np.uint8) & 0xF
        words = (c[..., 0::2] | (c[..., 1::2] << 4)).reshape(k // 512, 128, 2 * n)
    return np.ascontiguousarray(words), np.ascontiguousarray(byte.astype(np.uint8).reshape(k // 512, 16, n))


def unpack_weight(words, scales, fmt):
    g, _, n = scales.shape
    words = np.ascontiguousarray(words).reshape(g, 128, n, -1)
    if fmt in ("e4m3", "e5m2"):
        vals = words.view(ml_dtypes.float8_e4m3fn if fmt == "e4m3" else ml_dtypes.float8_e5m2).astype(np.float64)
    else:
        nib = np.empty((g, 128, n, 4), np.uint8)
        nib[..., 0::2] = words & 0xF
        nib[..., 1::2] = words >> 4
        vals = E2M1[nib]
    vals = vals * np.repeat(np.exp2(scales.astype(np.float64) - 127.0), 8, axis=1)[..., None]
    return vals.transpose(0, 1, 3, 2).reshape(g * 512, n)


def sigmoid(v):
    return 1.0 / (1.0 + np.exp(-v))


K, T, J, R, C, O, N, S, E = 512, 1024, 256, 512, 512, 128, 256, 1024, 512


def setup_inputs():
    n = np.random.standard_normal
    idx = np.random.permutation(T)[:J]
    idx2 = np.random.permutation(C)[:J]
    idx3 = np.random.permutation(C)[:O]
    idx4 = np.random.permutation(J)[:O]
    idx5 = np.random.permutation(S)[:N]
    idx6 = np.random.permutation(E)[:O]
    fk = mx_kscale(K)
    fr = mx_kscale(R)
    xtp = pack_weight(n((K, T)) / fk[:, None], "e5m2")
    wp = pack_weight(n((K, R)) * 1 / np.sqrt(K) * fk[:, None], "e2m1")
    w2p = pack_weight(n((K, R)) * 1 / np.sqrt(K) * fk[:, None] * fr, "e4m3")
    vsp = pack_weight(n((R, S)) * 1 / np.sqrt(R) / fr[:, None], "e2m1")
    return {
        "xt_words": xtp[0],
        "xt_scales": xtp[1],
        "w_words": wp[0],
        "w_scales": wp[1],
        "w2_words": w2p[0],
        "w2_scales": w2p[1],
        "sg": (np.random.uniform(0.6, 1.6, (R, 1))).astype(np.float32),
        "bg": (np.random.uniform(-1.0, 1.0, (R, 1))).astype(np.float32),
        "vs_words": vsp[0],
        "vs_scales": vsp[1],
        "tz": (n((N, E))).astype(np.float32),
        "so": (np.random.uniform(0.6, 1.6, (N, 1))).astype(np.float32),
        "bo": (np.random.uniform(-1.0, 1.0, (N, 1))).astype(np.float32),
        "offs": striped(idx),
        "offs2": striped(idx2),
        "offs3": striped(idx3),
        "offs4": striped(idx4),
        "offs5": striped(idx5),
        "offs6": striped(idx6),
    }


def reference(xt_words, xt_scales, w_words, w_scales, w2_words, w2_scales, sg, bg, vs_words, vs_scales, tz, so, bo, offs, offs2, offs3, offs4, offs5, offs6):
    idx = unstriped(offs)
    idx2 = unstriped(offs2)
    idx3 = unstriped(offs3)
    idx4 = unstriped(offs4)
    idx5 = unstriped(offs5)
    idx6 = unstriped(offs6)
    xtu = unpack_weight(xt_words, xt_scales, "e5m2")
    wu = unpack_weight(w_words, w_scales, "e2m1")
    w2u = unpack_weight(w2_words, w2_scales, "e4m3")
    vsu = unpack_weight(vs_words, vs_scales, "e2m1")
    xtidxg = xtu[:, idx]
    a = wu.T @ xtidxg
    b = w2u.T @ xtidxg
    pw = np.zeros((R, C))
    pw[:, idx2] = b
    hid = pw[:, idx3] * sigmoid(a[:, idx4] * f64(sg) + f64(bg))
    vsidx5g = vsu[:, idx5]
    hidq = mxq(hid, 0, "e4m3")
    p = vsidx5g.T @ hidq
    y = p * sigmoid(f64(tz)[:, idx6] * f64(so) + f64(bo))
    return y

@@ -1,0 +1,175 @@
+from contextlib import ExitStack
+
+import concourse.mybir as mybir
+
+K, T, J, R, C, O, N, S, E = 512, 1024, 256, 512, 512, 128, 256, 1024, 512
+FLOPS = 2 * K * R * J * 2 + 2 * R * N * O
+
+F32 = mybir.dt.float32
+BF16 = mybir.dt.bfloat16
+I32 = mybir.dt.int32
+U32 = mybir.dt.uint32
+U16 = mybir.dt.uint16
+U8 = mybir.dt.uint8
+E4M3 = mybir.dt.float8_e4m3fn_x4
+E5M2 = mybir.dt.float8_e5m2_x4
+E2M1 = mybir.dt.float4_e2m1fn_x4
+ACT = mybir.ActivationFunctionType
+MULT = mybir.AluOpType.mult
+
+P = 128
+PACK = 4
+HALVES = N // P
+
+
+def tile_list_gatedboard_twow_store_finalgate_kernel(
+    tc, xt_words, xt_scales, w_words, w_scales, w2_words, w2_scales, sg, bg, vs_words, vs_scales,
+    tz, so, bo, offs, offs2, offs3, offs4, offs5, offs6, out,
+):
+    nc = tc.nc
+    with ExitStack() as ctx:
+        pool = ctx.enter_context(tc.tile_pool(name="sb", bufs=1))
+        psum = ctx.enter_context(tc.psum_pool(name="ps", bufs=1))
+
+        def sb(name, shape, dtype):
+            return pool.tile(shape, dtype, name=name, align_bytes=64)
+
+        def load_list(name, src):
+            tile = sb(name, list(src.shape), U16)
+            nc.sync.dma_start(tile[:], src)
+            return tile
+
+        def load_scale_rows(queue, plane, src, q):
+            rows = src[0, 4 * q : 4 * q + 4, :].bitcast(I32)
+            queue.dma_start(plane[32 * q : 32 * q + 32, :].bitcast(I32), rows.partition_broadcast(8))
+
+        x_plane = sb("x_plane", [P, T], U8)
+        w2_plane = sb("w2_plane", [P, R], U8)
+        w_plane = sb("w_plane", [P, R], U8)
+        v_plane = sb("v_plane", [P, S], U8)
+        boards = [sb("board%d" % t, [P, C], F32) for t in range(PACK)]
+        for board in boards:
+            nc.vector.memset(board[:], 0.0)
+
+        x_table = sb("x_table", [P, T], U32)
+        w2_raw = sb("w2_raw", [P, R], U32)
+        w_raw = sb("w_raw", [P, R], U16)
+        v_table = sb("v_table", [P, S], U16)
+        tz_rows = [sb("tz%d" % h, [P, E], F32) for h in range(HALVES)]
+        sg_t = sb("sg_t", [P, PACK], F32)
+        bg_t = sb("bg_t", [P, PACK], F32)
+        so_t = sb("so_t", [P, HALVES], F32)
+        bo_t = sb("bo_t", [P, HALVES], F32)
+
+        tokens = load_list("tokens", offs)
+        for q in (0, 1):
+            load_scale_rows(nc.sync, x_plane, xt_scales, q)
+        nc.sync.dma_start(x_table[:].bitcast(I32), xt_words[0].rearrange("p c r -> p (c r)").bitcast(I32))
+        nc.sync.dma_start(w2_raw[:].bitcast(I32), w2_words[0].rearrange("p c r -> p (c r)").bitcast(I32))
+        for q in (2, 3):
+            load_scale_rows(nc.sync, x_plane, xt_scales, q)
+        for q in range(4):
+            load_scale_rows(nc.sync, w2_plane, w2_scales, q)
+        put_at = load_list("put_at", offs2)
+        nc.sync.dma_start(w_raw[:].bitcast(I32), w_words[0].bitcast(I32))
+        for q in range(4):
+            load_scale_rows(nc.sync, w_plane, w_scales, q)
+        entries = load_list("entries", offs5)
+        nc.sync.dma_start(v_table[:].bitcast(I32), vs_words[0].bitcast(I32))
+        slots = load_list("slots", offs4)
+        read_at = load_list("read_at", offs3)
+        gate_at = load_list("gate_at", offs6)
+        for h in range(HALVES):
+            nc.sync.dma_start(tz_rows[h][:], tz[h * P : (h + 1) * P, :])
+        for q in range(4):
+            load_scale_rows(nc.gpsimd, v_plane, vs_scales, q)
+        nc.gpsimd.dma_start(sg_t[:], sg.rearrange("(p t) o -> p (t o)", t=PACK))
+        nc.gpsimd.dma_start(bg_t[:], bg.rearrange("(p t) o -> p (t o)", t=PACK))
+        with nc.allow_non_contiguous_dma(reason="one float a partition for each half of the output features"):
+            nc.gpsimd.dma_start(so_t[:], so.rearrange("(h p) o -> p (h o)", p=P))
+            nc.gpsimd.dma_start(bo_t[:], bo.rearrange("(h p) o -> p (h o)", p=P))
+
+        def deal(copy, dst, src):
+            copy(out=dst[:].rearrange("p (t m) -> p m t", t=PACK), in_=src[:].rearrange("p (m t) -> p m t", t=PACK))
+
+        x_scale = sb("x_scale", [P, J], U8)
+        x_codes = sb("x_codes", [P, J], U32)
+        w2_codes = sb("w2_codes", [P, R], U32)
+        w2_scale = sb("w2_scale", [P, R], U8)
+        w_codes = sb("w_codes", [P, R], U16)
+        w_scale = sb("w_scale", [P, R], U8)
+        nc.vector.tensor_copy(x_scale[:], x_plane[:].indirect(tokens[:]))
+        nc.vector.tensor_copy(x_codes[:], x_table[:].indirect(tokens[:]))
+        deal(nc.scalar.copy, w2_codes, w2_raw)
+        deal(nc.vector.tensor_copy, w2_scale, w2_plane)
+
+        def first_stage(bank, codes, scale, fmt, t):
+            cols = slice(t * P, (t + 1) * P)
+            acc = psum.tile([P, J], F32, name=bank, tag=bank)
+            nc.tensor.matmul_mx(
+                out=acc[:], lhsT=codes[:, cols].bitcast(fmt), lhsT_scale=scale[:, cols],
+                rhs=x_codes[:].bitcast(E5M2), rhs_scale=x_scale[:], start=True, stop=True,
+            )
+            return acc
+
+        b_acc = [first_stage("bank%d" % t, w2_codes, w2_scale, E4M3, t) for t in range(PACK)]
+        deal(nc.scalar.copy, w_codes, w_raw)
+        deal(nc.vector.tensor_copy, w_scale, w_plane)
+        a_acc = [first_stage("bank%d" % (PACK + t), w_codes, w_scale, E2M1, t) for t in range(PACK)]
+        b_rows = [sb(name, [P, J], F32) for name in ("b0", "b1", "w_plane", "w_raw")]
+        picked = sb("picked", [P, PACK, O], F32)
+        gates = sb("gates", [P, PACK, O], F32)
+        v_codes = sb("v_codes", [P, N], U16)
+        v_scale = sb("v_scale", [P, N], U8)
+
+        def gate(t):
+            nc.scalar.activation(
+                gates[:, t, :], a_rows[t][:].indirect(slots[:]), ACT.Sigmoid,
+                bias=bg_t[:, t : t + 1], scale=sg_t[:, t : t + 1],
+            )
+
+        for t in (0, 2):
+            nc.vector.tensor_copy(b_rows[t][:], b_acc[t][:])
+            nc.scalar.copy(b_rows[t + 1][:], b_acc[t + 1][:])
+            nc.vector.tensor_copy(boards[t][:].indirect(put_at[:]), b_rows[t][:])
+            nc.scalar.activation(boards[t + 1][:].indirect(put_at[:]), b_rows[t + 1][:], ACT.Copy)
+        nc.vector.tensor_copy(v_codes[:], v_table[:].indirect(entries[:]))
+        nc.vector.tensor_copy(v_scale[:], v_plane[:].indirect(entries[:]))
+        a_rows = [sb(name, [P, J], F32) for name in ("v_table", "v_plane", "a2", "a3")]
+        for t in (0, 1):
+            nc.vector.tensor_copy(a_rows[t][:], a_acc[t][:])
+            nc.scalar.copy(a_rows[t + 2][:], a_acc[t + 2][:])
+        nc.scalar.activation(picked[:, 1, :], boards[1][:].indirect(read_at[:]), ACT.Copy)
+        for t in (0, 2, 3):
+            nc.vector.tensor_copy(picked[:, t, :], boards[t][:].indirect(read_at[:]))
+        for t in (2, 3, 0, 1):
+            gate(t)
+
+        hid_bf = sb("hid_bf", [P, O, PACK], BF16)
+        nc.vector.tensor_tensor(
+            hid_bf[:].rearrange("p (c i) t -> p c t i", i=4),
+            picked[:].rearrange("p t (c i) -> p c t i", i=4),
+            gates[:].rearrange("p t (c i) -> p c t i", i=4),
+            MULT,
+        )
+        h_codes = sb("h_codes", [P, O], U32)
+        h_scale = sb("h_scale", [P, O], U8)
+        nc.vector.quantize_mx(
+            out=h_codes[:].bitcast(E4M3), scales=h_scale[:], in_=hid_bf[:].rearrange("p o t -> p (o t)")
+        )
+
+        for h in range(HALVES):
+            cols = slice(h * P, (h + 1) * P)
+            last_gate = sb(("v_table", "v_plane")[h], [P, O], F32)
+            nc.scalar.activation(
+                last_gate[:], tz_rows[h][:].indirect(gate_at[:]), ACT.Sigmoid,
+                bias=bo_t[:, h : h + 1], scale=so_t[:, h : h + 1],
+            )
+            acc = psum.tile([P, J], F32, name="bank%d" % h, tag="bank%d" % h)
+            nc.tensor.matmul_mx(
+                out=acc[:, 0:O], lhsT=v_codes[:, cols].bitcast(E2M1), lhsT_scale=v_scale[:, cols],
+                rhs=h_codes[:].bitcast(E4M3), rhs_scale=h_scale[:], start=True, stop=True,
+            )
+            y = sb("y%d" % h, [P, O], F32)
+            nc.vector.tensor_tensor(y[:], acc[:, 0:O], last_gate[:], MULT)
+            (nc.sync if h == 0 else nc.scalar).dma_start(out[cols, :], y[:])

@@ -43,6 +43,10 @@ def tile_list_gatedboard_twow_store_finalgate_kernel(
             rows = src[0, 4 * q : 4 * q + 4, :].bitcast(I32)
             queue.dma_start(plane[32 * q : 32 * q + 32, :].bitcast(I32), rows.partition_broadcast(8))
 
+        warm = sb("warm", [P, 2], F32)
+        nc.gpsimd.memset(warm[:, 0:1], 0.0)
+        warm_out = sb("warm_out", [P, 1], F32)
+        nc.scalar.activation(warm_out[:], warm[:, 0:1], ACT.Sigmoid)
         x_plane = sb("x_plane", [P, T], U8)
         w2_plane = sb("w2_plane", [P, R], U8)
         w_plane = sb("w_plane", [P, R], U8)

@@ -93,8 +93,8 @@ def tile_list_gatedboard_twow_store_finalgate_kernel(
             nc.gpsimd.dma_start(so_t[:], so.rearrange("(h p) o -> p (h o)", p=P))
             nc.gpsimd.dma_start(bo_t[:], bo.rearrange("(h p) o -> p (h o)", p=P))
 
-        def deal(copy, dst, src):
-            copy(out=dst[:].rearrange("p (t m) -> p m t", t=PACK), in_=src[:].rearrange("p (m t) -> p m t", t=PACK))
+        def deal(dst, src):
+            nc.vector.tensor_copy(dst[:].rearrange("p (t m) -> p t m", t=PACK), src[:].rearrange("p (m t) -> p t m", t=PACK))
 
         x_scale = sb("x_scale", [P, J], U8)
         x_codes = sb("x_codes", [P, J], U32)
@@ -104,8 +104,10 @@ def tile_list_gatedboard_twow_store_finalgate_kernel(
         w_scale = sb("w_scale", [P, R], U8)
         nc.vector.tensor_copy(x_scale[:], x_plane[:].indirect(tokens[:]))
         nc.vector.tensor_copy(x_codes[:], x_table[:].indirect(tokens[:]))
-        deal(nc.scalar.copy, w2_codes, w2_raw)
-        deal(nc.vector.tensor_copy, w2_scale, w2_plane)
+        nc.scalar.copy(
+            w2_codes[:].rearrange("p (t m) -> p m t", t=PACK), w2_raw[:].rearrange("p (m t) -> p m t", t=PACK)
+        )
+        deal(w2_scale, w2_plane)
 
         def first_stage(bank, codes, scale, fmt, t):
             cols = slice(t * P, (t + 1) * P)
@@ -117,56 +119,58 @@ def tile_list_gatedboard_twow_store_finalgate_kernel(
             return acc
 
         b_acc = [first_stage("bank%d" % t, w2_codes, w2_scale, E4M3, t) for t in range(PACK)]
-        deal(nc.scalar.copy, w_codes, w_raw)
-        deal(nc.vector.tensor_copy, w_scale, w_plane)
+        deal(w_codes, w_raw)
+        deal(w_scale, w_plane)
         a_acc = [first_stage("bank%d" % (PACK + t), w_codes, w_scale, E2M1, t) for t in range(PACK)]
-        b_rows = [sb(name, [P, J], F32) for name in ("b0", "b1", "w_plane", "w_raw")]
-        picked = sb("picked", [P, PACK, O], F32)
-        gates = sb("gates", [P, PACK, O], F32)
-        v_codes = sb("v_codes", [P, N], U16)
-        v_scale = sb("v_scale", [P, N], U8)
-
-        def gate(t):
-            nc.scalar.activation(
-                gates[:, t, :], a_rows[t][:].indirect(slots[:]), ACT.Sigmoid,
-                bias=bg_t[:, t : t + 1], scale=sg_t[:, t : t + 1],
-            )
-
+        b_rows = [sb(name, [P, J], F32) for name in ("b0", "b1", "w_plane", "b3")]
         for t in (0, 2):
             nc.vector.tensor_copy(b_rows[t][:], b_acc[t][:])
             nc.scalar.copy(b_rows[t + 1][:], b_acc[t + 1][:])
             nc.vector.tensor_copy(boards[t][:].indirect(put_at[:]), b_rows[t][:])
             nc.scalar.activation(boards[t + 1][:].indirect(put_at[:]), b_rows[t + 1][:], ACT.Copy)
+
+        v_codes = sb("v_codes", [P, N], U16)
+        v_scale = sb("v_scale", [P, N], U8)
         nc.vector.tensor_copy(v_codes[:], v_table[:].indirect(entries[:]))
         nc.vector.tensor_copy(v_scale[:], v_plane[:].indirect(entries[:]))
-        a_rows = [sb(name, [P, J], F32) for name in ("v_table", "v_plane", "a2", "a3")]
-        for t in (0, 1):
-            nc.vector.tensor_copy(a_rows[t][:], a_acc[t][:])
-            nc.scalar.copy(a_rows[t + 2][:], a_acc[t + 2][:])
-        nc.scalar.activation(picked[:, 1, :], boards[1][:].indirect(read_at[:]), ACT.Copy)
-        for t in (0, 2, 3):
-            nc.vector.tensor_copy(picked[:, t, :], boards[t][:].indirect(read_at[:]))
-        for t in (2, 3, 0, 1):
-            gate(t)
 
-        hid_bf = sb("hid_bf", [P, O, PACK], BF16)
-        nc.vector.tensor_tensor(
-            hid_bf[:].rearrange("p (c i) t -> p c t i", i=4),
-            picked[:].rearrange("p t (c i) -> p c t i", i=4),
-            gates[:].rearrange("p t (c i) -> p c t i", i=4),
-            MULT,
-        )
+        a_rows = [sb("a%d" % t, [P, J], F32) for t in range(PACK)]
+        gates = sb("gates", [P, PACK, O], F32)
+        picked = sb("v_table", [P, PACK, O], F32)
+        for t in range(PACK + 1):
+            if t < PACK:
+                nc.scalar.copy(a_rows[t][:], a_acc[t][:])
+            if t > 0:
+                u = t - 1
+                nc.scalar.activation(
+                    gates[:, u, :], a_rows[u][:].indirect(slots[:]), ACT.Sigmoid,
+                    bias=bg_t[:, u : u + 1], scale=sg_t[:, u : u + 1],
+                )
+        for t in (0, 2, 1, 3):
+            nc.vector.tensor_copy(picked[:, t, :], boards[t][:].indirect(read_at[:]))
+
+        hid_bf = sb("v_plane", [P, O, PACK], BF16)
         h_codes = sb("h_codes", [P, O], U32)
         h_scale = sb("h_scale", [P, O], U8)
-        nc.vector.quantize_mx(
-            out=h_codes[:].bitcast(E4M3), scales=h_scale[:], in_=hid_bf[:].rearrange("p o t -> p (o t)")
-        )
+        places = [slice(0, O // 2), slice(O // 2, O)]
+        for part in places:
+            nc.vector.tensor_tensor(
+                hid_bf[:, part, :].rearrange("p (c i) t -> p c t i", i=2),
+                picked[:, :, part].rearrange("p t (c i) -> p c t i", i=2),
+                gates[:, :, part].rearrange("p t (c i) -> p c t i", i=2),
+                MULT,
+            )
+        for part in places:
+            nc.vector.quantize_mx(
+                out=h_codes[:, part].bitcast(E4M3), scales=h_scale[:, part],
+                in_=hid_bf[:, part, :].rearrange("p o t -> p (o t)"),
+            )
 
+        last_gate = sb("a%d" % (PACK - 1), [P, HALVES, O], F32)
         for h in range(HALVES):
             cols = slice(h * P, (h + 1) * P)
-            last_gate = sb(("v_table", "v_plane")[h], [P, O], F32)
             nc.scalar.activation(
-                last_gate[:], tz_rows[h][:].indirect(gate_at[:]), ACT.Sigmoid,
+                last_gate[:, h, :], tz_rows[h][:].indirect(gate_at[:]), ACT.Sigmoid,
                 bias=bo_t[:, h : h + 1], scale=so_t[:, h : h + 1],
             )
             acc = psum.tile([P, J], F32, name="bank%d" % h, tag="bank%d" % h)
@@ -175,5 +179,5 @@ def tile_list_gatedboard_twow_store_finalgate_kernel(
                 rhs=h_codes[:].bitcast(E4M3), rhs_scale=h_scale[:], start=True, stop=True,
             )
             y = sb("y%d" % h, [P, O], F32)
-            nc.vector.tensor_tensor(y[:], acc[:, 0:O], last_gate[:], MULT)
+            nc.vector.tensor_tensor(y[:], acc[:, 0:O], last_gate[:, h, :], MULT)
             (nc.sync if h == 0 else nc.scalar).dma_start(out[cols, :], y[:])

@@ -66,12 +66,10 @@ def tile_list_gatedboard_twow_store_finalgate_kernel(
         bo_t = sb("bo_t", [P, HALVES], F32)
 
         tokens = load_list("tokens", offs)
-        for q in (0, 1):
+        for q in range(4):
             load_scale_rows(nc.sync, x_plane, xt_scales, q)
         nc.sync.dma_start(x_table[:].bitcast(I32), xt_words[0].rearrange("p c r -> p (c r)").bitcast(I32))
         nc.sync.dma_start(w2_raw[:].bitcast(I32), w2_words[0].rearrange("p c r -> p (c r)").bitcast(I32))
-        for q in (2, 3):
-            load_scale_rows(nc.sync, x_plane, xt_scales, q)
         for q in range(4):
             load_scale_rows(nc.sync, w2_plane, w2_scales, q)
         put_at = load_list("put_at", offs2)
@@ -81,14 +79,14 @@ def tile_list_gatedboard_twow_store_finalgate_kernel(
         entries = load_list("entries", offs5)
         nc.sync.dma_start(v_table[:].bitcast(I32), vs_words[0].bitcast(I32))
         slots = load_list("slots", offs4)
+        nc.sync.dma_start(sg_t[:], sg.rearrange("(p t) o -> p (t o)", t=PACK))
+        nc.sync.dma_start(bg_t[:], bg.rearrange("(p t) o -> p (t o)", t=PACK))
         read_at = load_list("read_at", offs3)
         gate_at = load_list("gate_at", offs6)
         for h in range(HALVES):
             nc.sync.dma_start(tz_rows[h][:], tz[h * P : (h + 1) * P, :])
         for q in range(4):
             load_scale_rows(nc.gpsimd, v_plane, vs_scales, q)
-        nc.gpsimd.dma_start(sg_t[:], sg.rearrange("(p t) o -> p (t o)", t=PACK))
-        nc.gpsimd.dma_start(bg_t[:], bg.rearrange("(p t) o -> p (t o)", t=PACK))
         with nc.allow_non_contiguous_dma(reason="one float a partition for each half of the output features"):
             nc.gpsimd.dma_start(so_t[:], so.rearrange("(h p) o -> p (h o)", p=P))
             nc.gpsimd.dma_start(bo_t[:], bo.rearrange("(h p) o -> p (h o)", p=P))
@@ -104,10 +102,15 @@ def tile_list_gatedboard_twow_store_finalgate_kernel(
         w_scale = sb("w_scale", [P, R], U8)
         nc.vector.tensor_copy(x_scale[:], x_plane[:].indirect(tokens[:]))
         nc.vector.tensor_copy(x_codes[:], x_table[:].indirect(tokens[:]))
-        nc.scalar.copy(
-            w2_codes[:].rearrange("p (t m) -> p m t", t=PACK), w2_raw[:].rearrange("p (m t) -> p m t", t=PACK)
-        )
-        deal(w2_scale, w2_plane)
+        for pair in (slice(0, 2), slice(2, 4)):
+            nc.scalar.copy(
+                w2_codes[:].rearrange("p (t m) -> p m t", t=PACK)[:, :, pair],
+                w2_raw[:].rearrange("p (m t) -> p m t", t=PACK)[:, :, pair],
+            )
+            nc.vector.tensor_copy(
+                w2_scale[:].rearrange("p (t m) -> p t m", t=PACK)[:, pair, :],
+                w2_plane[:].rearrange("p (m t) -> p t m", t=PACK)[:, pair, :],
+            )
 
         def first_stage(bank, codes, scale, fmt, t):
             cols = slice(t * P, (t + 1) * P)
@@ -118,16 +121,19 @@ def tile_list_gatedboard_twow_store_finalgate_kernel(
             )
             return acc
 
-        b_acc = [first_stage("bank%d" % t, w2_codes, w2_scale, E4M3, t) for t in range(PACK)]
+        b_acc = {t: first_stage("bank%d" % t, w2_codes, w2_scale, E4M3, t) for t in (0, 1, 3, 2)}
         deal(w_codes, w_raw)
         deal(w_scale, w_plane)
         a_acc = [first_stage("bank%d" % (PACK + t), w_codes, w_scale, E2M1, t) for t in range(PACK)]
         b_rows = [sb(name, [P, J], F32) for name in ("b0", "b1", "w_plane", "b3")]
-        for t in (0, 2):
-            nc.vector.tensor_copy(b_rows[t][:], b_acc[t][:])
-            nc.scalar.copy(b_rows[t + 1][:], b_acc[t + 1][:])
-            nc.vector.tensor_copy(boards[t][:].indirect(put_at[:]), b_rows[t][:])
-            nc.scalar.activation(boards[t + 1][:].indirect(put_at[:]), b_rows[t + 1][:], ACT.Copy)
+        nc.vector.tensor_copy(b_rows[0][:], b_acc[0][:])
+        for t in (1, 3):
+            nc.scalar.copy(b_rows[t][:], b_acc[t][:])
+        nc.vector.tensor_copy(boards[0][:].indirect(put_at[:]), b_rows[0][:])
+        for t in (1, 3):
+            nc.scalar.activation(boards[t][:].indirect(put_at[:]), b_rows[t][:], ACT.Copy)
+        nc.vector.tensor_copy(b_rows[2][:], b_acc[2][:])
+        nc.vector.tensor_copy(boards[2][:].indirect(put_at[:]), b_rows[2][:])
 
         v_codes = sb("v_codes", [P, N], U16)
         v_scale = sb("v_scale", [P, N], U8)
@@ -146,7 +152,9 @@ def tile_list_gatedboard_twow_store_finalgate_kernel(
                     gates[:, u, :], a_rows[u][:].indirect(slots[:]), ACT.Sigmoid,
                     bias=bg_t[:, u : u + 1], scale=sg_t[:, u : u + 1],
                 )
-        for t in (0, 2, 1, 3):
+        for t in (1, 3):
+            nc.scalar.activation(picked[:, t, :], boards[t][:].indirect(read_at[:]), ACT.Copy)
+        for t in (0, 2):
             nc.vector.tensor_copy(picked[:, t, :], boards[t][:].indirect(read_at[:]))
 
         hid_bf = sb("v_plane", [P, O, PACK], BF16)

from contextlib import ExitStack

import concourse.mybir as mybir

K, T, J, R, C, O, N, S, E = 512, 1024, 256, 512, 512, 128, 256, 1024, 512
FLOPS = 2 * K * R * J * 2 + 2 * R * N * O

F32 = mybir.dt.float32
BF16 = mybir.dt.bfloat16
I32 = mybir.dt.int32
U32 = mybir.dt.uint32
U16 = mybir.dt.uint16
U8 = mybir.dt.uint8
E4M3 = mybir.dt.float8_e4m3fn_x4
E5M2 = mybir.dt.float8_e5m2_x4
E2M1 = mybir.dt.float4_e2m1fn_x4
ACT = mybir.ActivationFunctionType
MULT = mybir.AluOpType.mult

P = 128
PACK = 4
HALVES = N // P


def tile_list_gatedboard_twow_store_finalgate_kernel(
    tc, xt_words, xt_scales, w_words, w_scales, w2_words, w2_scales, sg, bg, vs_words, vs_scales,
    tz, so, bo, offs, offs2, offs3, offs4, offs5, offs6, out,
):
    nc = tc.nc
    with ExitStack() as ctx:
        pool = ctx.enter_context(tc.tile_pool(name="sb", bufs=1))
        psum = ctx.enter_context(tc.psum_pool(name="ps", bufs=1))

        def sb(name, shape, dtype):
            return pool.tile(shape, dtype, name=name, align_bytes=64)

        def load_list(name, src):
            tile = sb(name, list(src.shape), U16)
            nc.sync.dma_start(tile[:], src)
            return tile

        def load_scale_rows(queue, plane, src, q):
            rows = src[0, 4 * q : 4 * q + 4, :].bitcast(I32)
            queue.dma_start(plane[32 * q : 32 * q + 32, :].bitcast(I32), rows.partition_broadcast(8))

        warm = sb("warm", [P, 2], F32)
        nc.gpsimd.memset(warm[:, 0:1], 0.0)
        warm_out = sb("warm_out", [P, 1], F32)
        nc.scalar.activation(warm_out[:], warm[:, 0:1], ACT.Sigmoid)
        x_plane = sb("x_plane", [P, T], U8)
        w2_plane = sb("w2_plane", [P, R], U8)
        w_plane = sb("w_plane", [P, R], U8)
        v_plane = sb("v_plane", [P, S], U8)
        boards = [sb("board%d" % t, [P, C], F32) for t in range(PACK)]
        for board in boards:
            nc.vector.memset(board[:], 0.0)

        x_table = sb("x_table", [P, T], U32)
        w2_raw = sb("w2_raw", [P, R], U32)
        w_raw = sb("w_raw", [P, R], U16)
        v_table = sb("v_table", [P, S], U16)
        tz_rows = [sb("tz%d" % h, [P, E], F32) for h in range(HALVES)]
        sg_t = sb("sg_t", [P, PACK], F32)
        bg_t = sb("bg_t", [P, PACK], F32)
        so_t = sb("so_t", [P, HALVES], F32)
        bo_t = sb("bo_t", [P, HALVES], F32)

        tokens = load_list("tokens", offs)
        for q in range(4):
            load_scale_rows(nc.sync, x_plane, xt_scales, q)
        nc.sync.dma_start(x_table[:].bitcast(I32), xt_words[0].rearrange("p c r -> p (c r)").bitcast(I32))
        nc.sync.dma_start(w2_raw[:].bitcast(I32), w2_words[0].rearrange("p c r -> p (c r)").bitcast(I32))
        for q in range(4):
            load_scale_rows(nc.sync, w2_plane, w2_scales, q)
        put_at = load_list("put_at", offs2)
        nc.sync.dma_start(w_raw[:].bitcast(I32), w_words[0].bitcast(I32))
        for q in range(4):
            load_scale_rows(nc.sync, w_plane, w_scales, q)
        entries = load_list("entries", offs5)
        nc.sync.dma_start(v_table[:].bitcast(I32), vs_words[0].bitcast(I32))
        slots = load_list("slots", offs4)
        nc.sync.dma_start(sg_t[:], sg.rearrange("(p t) o -> p (t o)", t=PACK))
        nc.sync.dma_start(bg_t[:], bg.rearrange("(p t) o -> p (t o)", t=PACK))
        read_at = load_list("read_at", offs3)
        gate_at = load_list("gate_at", offs6)
        for h in range(HALVES):
            nc.sync.dma_start(tz_rows[h][:], tz[h * P : (h + 1) * P, :])
        for q in range(4):
            load_scale_rows(nc.gpsimd, v_plane, vs_scales, q)
        with nc.allow_non_contiguous_dma(reason="one float a partition for each half of the output features"):
            nc.gpsimd.dma_start(so_t[:], so.rearrange("(h p) o -> p (h o)", p=P))
            nc.gpsimd.dma_start(bo_t[:], bo.rearrange("(h p) o -> p (h o)", p=P))

        def deal(dst, src):
            nc.vector.tensor_copy(dst[:].rearrange("p (t m) -> p t m", t=PACK), src[:].rearrange("p (m t) -> p t m", t=PACK))

        x_scale = sb("x_scale", [P, J], U8)
        x_codes = sb("x_codes", [P, J], U32)
        w2_codes = sb("w2_codes", [P, R], U32)
        w2_scale = sb("w2_scale", [P, R], U8)
        w_codes = sb("w_codes", [P, R], U16)
        w_scale = sb("w_scale", [P, R], U8)
        nc.vector.tensor_copy(x_scale[:], x_plane[:].indirect(tokens[:]))
        nc.vector.tensor_copy(x_codes[:], x_table[:].indirect(tokens[:]))
        for pair in (slice(0, 2), slice(2, 4)):
            nc.scalar.copy(
                w2_codes[:].rearrange("p (t m) -> p m t", t=PACK)[:, :, pair],
                w2_raw[:].rearrange("p (m t) -> p m t", t=PACK)[:, :, pair],
            )
            nc.vector.tensor_copy(
                w2_scale[:].rearrange("p (t m) -> p t m", t=PACK)[:, pair, :],
                w2_plane[:].rearrange("p (m t) -> p t m", t=PACK)[:, pair, :],
            )

        def first_stage(bank, codes, scale, fmt, t):
            cols = slice(t * P, (t + 1) * P)
            acc = psum.tile([P, J], F32, name=bank, tag=bank)
            nc.tensor.matmul_mx(
                out=acc[:], lhsT=codes[:, cols].bitcast(fmt), lhsT_scale=scale[:, cols],
                rhs=x_codes[:].bitcast(E5M2), rhs_scale=x_scale[:], start=True, stop=True,
            )
            return acc

        b_acc = {t: first_stage("bank%d" % t, w2_codes, w2_scale, E4M3, t) for t in (0, 1, 3, 2)}
        deal(w_codes, w_raw)
        deal(w_scale, w_plane)
        a_acc = [first_stage("bank%d" % (PACK + t), w_codes, w_scale, E2M1, t) for t in range(PACK)]
        b_rows = [sb(name, [P, J], F32) for name in ("b0", "b1", "w_plane", "b3")]
        nc.vector.tensor_copy(b_rows[0][:], b_acc[0][:])
        for t in (1, 3):
            nc.scalar.copy(b_rows[t][:], b_acc[t][:])
        nc.vector.tensor_copy(boards[0][:].indirect(put_at[:]), b_rows[0][:])
        for t in (1, 3):
            nc.scalar.activation(boards[t][:].indirect(put_at[:]), b_rows[t][:], ACT.Copy)
        nc.vector.tensor_copy(b_rows[2][:], b_acc[2][:])
        nc.vector.tensor_copy(boards[2][:].indirect(put_at[:]), b_rows[2][:])

        v_codes = sb("v_codes", [P, N], U16)
        v_scale = sb("v_scale", [P, N], U8)
        nc.vector.tensor_copy(v_codes[:], v_table[:].indirect(entries[:]))
        nc.vector.tensor_copy(v_scale[:], v_plane[:].indirect(entries[:]))

        a_rows = [sb("a%d" % t, [P, J], F32) for t in range(PACK)]
        gates = sb("gates", [P, PACK, O], F32)
        picked = sb("v_table", [P, PACK, O], F32)
        for t in range(PACK + 1):
            if t < PACK:
                nc.scalar.copy(a_rows[t][:], a_acc[t][:])
            if t > 0:
                u = t - 1
                nc.scalar.activation(
                    gates[:, u, :], a_rows[u][:].indirect(slots[:]), ACT.Sigmoid,
                    bias=bg_t[:, u : u + 1], scale=sg_t[:, u : u + 1],
                )
        for t in (1, 3):
            nc.scalar.activation(picked[:, t, :], boards[t][:].indirect(read_at[:]), ACT.Copy)
        for t in (0, 2):
            nc.vector.tensor_copy(picked[:, t, :], boards[t][:].indirect(read_at[:]))

        hid_bf = sb("v_plane", [P, O, PACK], BF16)
        h_codes = sb("h_codes", [P, O], U32)
        h_scale = sb("h_scale", [P, O], U8)
        places = [slice(0, O // 2), slice(O // 2, O)]
        for part in places:
            nc.vector.tensor_tensor(
                hid_bf[:, part, :].rearrange("p (c i) t -> p c t i", i=2),
                picked[:, :, part].rearrange("p t (c i) -> p c t i", i=2),
                gates[:, :, part].rearrange("p t (c i) -> p c t i", i=2),
                MULT,
            )
        for part in places:
            nc.vector.quantize_mx(
                out=h_codes[:, part].bitcast(E4M3), scales=h_scale[:, part],
                in_=hid_bf[:, part, :].rearrange("p o t -> p (o t)"),
            )

        last_gate = sb("a%d" % (PACK - 1), [P, HALVES, O], F32)
        for h in range(HALVES):
            cols = slice(h * P, (h + 1) * P)
            nc.scalar.activation(
                last_gate[:, h, :], tz_rows[h][:].indirect(gate_at[:]), ACT.Sigmoid,
                bias=bo_t[:, h : h + 1], scale=so_t[:, h : h + 1],
            )
            acc = psum.tile([P, J], F32, name="bank%d" % h, tag="bank%d" % h)
            nc.tensor.matmul_mx(
                out=acc[:, 0:O], lhsT=v_codes[:, cols].bitcast(E2M1), lhsT_scale=v_scale[:, cols],
                rhs=h_codes[:].bitcast(E4M3), rhs_scale=h_scale[:], start=True, stop=True,
            )
            y = sb("y%d" % h, [P, O], F32)
            nc.vector.tensor_tensor(y[:], acc[:, 0:O], last_gate[:, h, :], MULT)
            (nc.sync if h == 0 else nc.scalar).dma_start(out[cols, :], y[:])
